import numpy as np
import ml_dtypes


def mxq(x, axis, fmt="e4m3"):
    dtype, down = {"e4m3": (ml_dtypes.float8_e4m3fn, 7), "e5m2": (ml_dtypes.float8_e5m2, 14)}[fmt]
    v = np.moveaxis(np.asarray(x, np.float32).astype(ml_dtypes.bfloat16).astype(np.float64), axis, -1)
    blocks = v.reshape(v.shape[:-1] + (-1, 32))
    amax = np.abs(blocks).max(-1, keepdims=True)
    byte = np.maximum(np.where(amax > 0, np.frexp(amax)[1] - 1 + 127, 0) - down, 1)
    scale = np.exp2(byte - 127.0)
    codes = (blocks / scale).astype(np.float32).astype(dtype).astype(np.float64)
    return np.moveaxis((codes * scale).reshape(v.shape), -1, axis)


WIDE = False


def mx_kscale(k):
    if not WIDE:
        return np.ones(k)
    levels = np.array([10, -10, 5, -5, 0])
    if k % 512:
        return np.exp2(np.random.permutation(np.resize(levels, k // 32))).repeat(32)
    a = np.empty((k // 512, 16))
    for p in range(k // 512):
        a[p, :8] = np.random.permutation(np.resize(levels, 8))
        for g in range(8):
            far = levels[np.abs(levels - a[p, g]) >= 10]
            a[p, g + 8] = far[np.random.randint(len(far))]
    return np.exp2(a.ravel()).repeat(32)


def f64(x):
    return np.asarray(x).astype(np.float64)


def striped(idx):
    return np.tile(idx.reshape(-1, 16).T, (8, 1)).astype(np.uint16)


def unstriped(offs):
    return offs[:16].T.reshape(-1).astype(np.int64)


def pack_weight(w):
    k, n = w.shape
    w = f64(np.asarray(w, np.float32).astype(ml_dtypes.bfloat16)).reshape(k // 32, 32, n)
    amax = np.abs(w).max(1)
    byte = np.clip(np.where(amax > 0, np.frexp(amax)[1] - 1 + 127 - 7, 1), 1, 254)
    scaled = (w * np.exp2(127.0 - byte)[:, None, :]).reshape(k, n).astype(np.float32)
    words = np.ascontiguousarray(scaled.reshape(k // 512, 128, 4, n).transpose(0, 1, 3, 2)).astype(ml_dtypes.float8_e4m3fn).view(np.uint8)
    return words, np.ascontiguousarray(byte.astype(np.uint8).reshape(k // 512, 16, n))


def unpack_weight(words, scales):
    g, p, n, _ = words.shape
    vals = np.ascontiguousarray(words).view(ml_dtypes.float8_e4m3fn).astype(np.float64) * np.repeat(np.exp2(scales.astype(np.float64) - 127.0), 8, axis=1)[..., None]
    return vals.transpose(0, 1, 3, 2).reshape(g * 512, n)


K, T, S, V, H, J, W, G = 512, 2048, 512, 512, 512, 512, 256, 2048


def setup_inputs():
    n = np.random.standard_normal
    s = mx_kscale(K)[:, None]
    u = mx_kscale(S)
    packed_xT = pack_weight(n((K, T)) * s)
    perm = np.random.permutation(V)
    return {
        "x_words": packed_xT[0],
        "x_scales": packed_xT[1],
        "w1": (n((K, H)) / np.sqrt(K) / s).astype(np.float32),
        "w2": (n((K, H)) / np.sqrt(K) / s).astype(np.float32),
        "tab": np.random.uniform(0.4, 1.4, (H, J)).astype(np.float32),
        "ga": (np.random.uniform(0.5, 1.5, (H, 1)) * u[:, None]).astype(np.float32),
        "gb": (np.random.uniform(0.5, 1.5, (H, 1)) / u[:, None]).astype(np.float32),
        "tau": np.random.uniform(0.3, 0.9, (S, 1)).astype(np.float32),
        "offs": striped(np.random.permutation(T)[:S]),
        "two": striped(np.random.permutation(T)[:V]),
        "n1": striped(np.random.randint(0, J, S)),
        "n2": striped(np.random.permutation(S)),
        "n3": striped(perm[:W]),
        "n4": striped(perm[W:]),
        "n5": striped(np.random.randint(0, V, G)),
    }


def reference(x_words, x_scales, w1, w2, tab, ga, gb, tau, offs, two, n1, n2, n3, n4, n5):
    xq = unpack_weight(x_words, x_scales)[:, unstriped(offs)]
    a = mxq(f64(w1), 0, "e4m3").T @ xq
    z = f64(ga) * (a * f64(tab)[:, unstriped(n1)] - (0.5 * a[:, unstriped(n2)]))
    x_two = unpack_weight(x_words, x_scales)[:, unstriped(two)]
    b = mxq(f64(w2), 0, "e4m3").T @ x_two
    pb = b[:, unstriped(n4)]
    pa = b[:, unstriped(n3)]
    rb = pb - (0.5 * pa)
    ra = np.sqrt((pa) ** 2 + (pb) ** 2 + 0.25)
    ds = np.zeros((H, V))
    ds[:, unstriped(n3)] = ra
    dt = ds.copy()
    dt[:, unstriped(n4)] = rb
    z2 = f64(gb) * dt
    s = 0.0625 * ((mxq(z, 0, "e4m3").T @ mxq(z2, 0, "e4m3")))
    top = s.max(axis=1, keepdims=True)
    ea = np.exp(f64(tau) * (s[:, unstriped(n5)] - top))
    ms = ea.reshape(S, V, 4).sum(axis=2)
    return (1.5 * s) / (ms + 0.5)

@@ -1,0 +1,306 @@
+from contextlib import ExitStack
+
+import concourse.mybir as mybir
+
+K, T, S, V, H, W, G = 512, 2048, 512, 512, 512, 256, 2048
+FLOPS = 2 * K * H * S + 2 * K * H * V + 2 * H * S * V
+
+F32 = mybir.dt.float32
+BF16 = mybir.dt.bfloat16
+I32 = mybir.dt.int32
+U32 = mybir.dt.uint32
+U16 = mybir.dt.uint16
+U8 = mybir.dt.uint8
+FP8X4 = mybir.dt.float8_e4m3fn_x4
+ALU = mybir.AluOpType
+ACT = mybir.ActivationFunctionType
+
+P = 128
+PACK = 4
+LIST = 16
+ROWS = S // P
+EXP_PIECE = 256
+
+
+def tile_picked_kqkindgpolaregs_none_p_kernel(
+    tc, x_words, x_scales, w1, w2, tab, ga, gb, tau, offs, two, n1, n2, n3, n4, n5, out
+):
+    nc = tc.nc
+    with ExitStack() as ctx:
+        lists = ctx.enter_context(tc.tile_pool(name="lists", bufs=1))
+        keep = ctx.enter_context(tc.tile_pool(name="keep", bufs=1))
+        ring = ctx.enter_context(tc.tile_pool(name="ring", bufs=2))
+        psum = ctx.enter_context(tc.psum_pool(name="psum", bufs=1))
+
+        def load_list(name, source):
+            tile = lists.tile([P, source.shape[1]], U16, name=name)
+            nc.sync.dma_start(tile[:], source)
+            return tile
+
+        def load_weight(name, source):
+            tile = keep.tile([P, PACK, H], F32, name=name)
+            nc.sync.dma_start(tile[:], source.rearrange("(p j) c -> p j c", j=PACK))
+            return tile
+
+        scale_table = keep.tile([P, T], U8, name="scale_table")
+        nc.gpsimd.memset(scale_table[:].bitcast(I32), 0)
+        w2_raw = load_weight("w2_raw", w2)
+        for q in range(4):
+            nc.sync.dma_start(
+                scale_table[32 * q : 32 * q + 4, :].bitcast(I32), x_scales[0, 4 * q : 4 * q + 4, :].bitcast(I32)
+            )
+        two_list = load_list("two_list", two)
+        offs_list = load_list("offs_list", offs)
+        word_table = keep.tile([P, T], U32, name="word_table")
+        nc.sync.dma_start(word_table[:].bitcast(I32), x_words[0].rearrange("p c r -> p (c r)").bitcast(I32))
+        n1_list = load_list("n1_list", n1)
+        tab_rows = tab.rearrange("(p t) c -> t p c", t=PACK)
+        tab_tiles = []
+        for t in range(PACK):
+            tile = keep.tile([P, H], F32, name="tab%d" % t)
+            nc.sync.dma_start(tile[:], tab_rows[t])
+            tab_tiles.append(tile)
+        n3_list = load_list("n3_list", n3)
+        n4_list = load_list("n4_list", n4)
+        n2_list = load_list("n2_list", n2)
+        w1_raw = load_weight("w1_raw", w1)
+        n5_list = load_list("n5_list", n5)
+        tau_tile = keep.tile([P, ROWS], F32, name="tau_tile")
+        with nc.allow_non_contiguous_dma(reason="one rate a partition"):
+            nc.sync.dma_start(tau_tile[:], tau.rearrange("(i p) o -> p (i o)", p=P))
+        ga_tile = keep.tile([P, PACK], F32, name="ga_tile")
+        nc.gpsimd.dma_start(ga_tile[:], ga.rearrange("(p t) o -> p (t o)", t=PACK))
+        gb_tile = keep.tile([P, PACK], F32, name="gb_tile")
+        nc.gpsimd.dma_start(gb_tile[:], gb.rearrange("(p t) o -> p (t o)", t=PACK))
+
+        def gather_scales(name, offsets):
+            tile = keep.tile([P, S], U8, name=name, align_bytes=64)
+            nc.vector.tensor_copy(tile[:], scale_table[:].indirect(offsets[:]))
+            return tile
+
+        def gather_words(name, offsets, pieces):
+            tile = keep.tile([P, S], U32, name=name, align_bytes=64)
+            for first in range(0, S, S // pieces):
+                columns = slice(first // LIST, (first + S // pieces) // LIST)
+                nc.vector.tensor_copy(tile[:, first : first + S // pieces], word_table[:].indirect(offsets[:, columns]))
+            return tile
+
+        def deal_weight(name, raw, copies):
+            dealt = keep.tile([P, PACK * H], BF16, name=name, tag=name, align_bytes=64)
+            view = dealt[:].rearrange("p (t m j) -> p m j t", t=PACK, j=PACK)
+            source = raw[:].rearrange("p j (m t) -> p m j t", t=PACK)
+            share = P // len(copies)
+            for h, copy in enumerate(copies):
+                copy(view[:, h * share : (h + 1) * share], source[:, h * share : (h + 1) * share])
+            return dealt
+
+        def quantise(name, values):
+            width = values.shape[1] // PACK
+            codes = keep.tile([P, width], U32, name=name + "_codes", align_bytes=64)
+            scales = keep.tile([P, width], U8, name=name + "_scales", align_bytes=64)
+            nc.vector.quantize_mx(out=codes[:].bitcast(FP8X4), scales=scales[:], in_=values)
+            return codes, scales
+
+        def product(bank, left, left_columns, right):
+            nc.tensor.matmul_mx(
+                out=bank[:],
+                lhsT=left[0][:, left_columns].bitcast(FP8X4),
+                lhsT_scale=left[1][:, left_columns],
+                rhs=right[0][:].bitcast(FP8X4),
+                rhs_scale=right[1][:],
+                start=True,
+                stop=True,
+            )
+
+        two_scales = gather_scales("two_scales", two_list)
+        w2_dealt = deal_weight("w2_dealt", w2_raw, [nc.scalar.copy, nc.vector.tensor_copy])
+        offs_scales = gather_scales("offs_scales", offs_list)
+        w2_mx = quantise("w2", w2_dealt[:])
+        x_two = (gather_words("two_words", two_list, 1), two_scales)
+        b_tiles = []
+        for t in range(PACK):
+            bank = psum.tile([P, V], F32, name="bank_b%d" % t)
+            product(bank, w2_mx, slice(t * P, (t + 1) * P), x_two)
+            b_tile = keep.tile([P, V], F32, name="b%d" % t)
+            nc.vector.tensor_copy(b_tile[:], bank[:])
+            b_tiles.append(b_tile)
+
+        pairs, mixed, placed = {}, {}, {}
+        roots = w2_dealt[:].bitcast(F32).rearrange("p (t c) -> p t c", t=PACK)
+
+        def fetch_pairs(t):
+            pairs[t] = keep.tile([P, 2 * W], F32, name="pairs%d" % t)
+            nc.scalar.activation(pairs[t][:, :W], b_tiles[t][:].indirect(n3_list[:]), ACT.Copy)
+            nc.scalar.activation(pairs[t][:, W:], b_tiles[t][:].indirect(n4_list[:]), ACT.Copy)
+
+        def mix_pairs(t):
+            squares = ring.tile([P, 2 * W], F32, name="squares")
+            nc.vector.tensor_tensor(squares[:], pairs[t][:], pairs[t][:], ALU.mult)
+            mixed[t] = keep.tile([P, W], F32, name="rb%d" % t)
+            nc.vector.scalar_tensor_tensor(mixed[t][:], pairs[t][:, :W], -0.5, pairs[t][:, W:], ALU.mult, ALU.add)
+            radicand = keep.tile([P, W], F32, name="radicand%d" % t)
+            nc.vector.scalar_tensor_tensor(radicand[:], squares[:, :W], 0.25, squares[:, W:], ALU.add, ALU.add)
+            return radicand
+
+        def place_mixed(t):
+            placed[t] = keep.tile([P, V], F32, name="dt%d" % t)
+            nc.scalar.activation(placed[t][:].indirect(n4_list[:]), mixed[t][:], ACT.Copy)
+
+        def root(t, radicand):
+            nc.scalar.activation(roots[:, t, :], radicand[:], ACT.Sqrt)
+
+        def place_roots(t):
+            nc.scalar.activation(placed[t][:].indirect(n3_list[:]), roots[:, t, :], ACT.Copy)
+
+        half_a = keep.tile([P, PACK * S], F32, name="half_a")
+        partner = keep.tile([P, PACK, S], F32, name="partner", tag="partner")
+
+        def project_a(t):
+            bank = psum.tile([P, S], F32, name="bank_a%d" % t)
+            product(bank, w1_mx, slice(t * P, (t + 1) * P), x_offs)
+            nc.vector.tensor_scalar(half_a[:, t * S : (t + 1) * S], bank[:], ga_tile[:, t : t + 1], -0.5, ALU.mult, ALU.mult)
+
+        def fetch_partner(t, first, count):
+            offsets = n2_list[:, first // LIST : (first + count) // LIST]
+            nc.vector.tensor_copy(partner[:, t, first : first + count], half_a[:, t * S : (t + 1) * S].indirect(offsets))
+
+        kinds = {}
+
+        def fetch_kinds(h, tag):
+            kinds[h] = keep.tile([P, PACK, S // 2], F32, name="kinds%d" % h, tag=tag, align_bytes=64)
+            offsets = n1_list[:, h * S // 2 // LIST : (h + 1) * S // 2 // LIST]
+            for t in range(PACK):
+                nc.scalar.activation(kinds[h][:, t, :], tab_tiles[t][:].indirect(offsets), ACT.Copy)
+
+        z_mx = {}
+
+        def make_z(i):
+            columns = slice(i * P, (i + 1) * P)
+            weighted = keep.tile([P, PACK, P], F32, name="weighted%d" % i, tag="weighted%d" % (i % 2))
+            nc.vector.scalar_tensor_tensor(
+                weighted[:], half_a[:].rearrange("p (t c) -> p t c", t=PACK)[:, :, columns], -2.0,
+                kinds[i // 2][:, :, (i % 2) * P : (i % 2 + 1) * P],
+                ALU.mult, ALU.mult,
+            )
+            z_block = keep.tile([P, PACK * P], BF16, name="z_block%d" % i, tag="z_block%d" % (i % 2), align_bytes=64)
+            nc.vector.tensor_tensor(
+                z_block[:].rearrange("p (c e t) -> p c t e", e=4, t=PACK),
+                weighted[:].rearrange("p t (c e) -> p c t e", e=4),
+                partner[:, :, columns].rearrange("p t (c e) -> p c t e", e=4),
+                ALU.add,
+            )
+            z_mx[i] = quantise("z_rows%d" % i, z_block[:])
+
+        fetch_kinds(0, "kinds0")
+        for t in range(PACK):
+            fetch_pairs(t)
+        for t in range(PACK):
+            radicand = mix_pairs(t)
+            place_mixed(t)
+            root(t, radicand)
+            if t > 0:
+                place_roots(t - 1)
+        place_roots(PACK - 1)
+        x_offs = (gather_words("offs_words", offs_list, 2), offs_scales)
+        w1_dealt = deal_weight("w1_dealt", w1_raw, [nc.vector.tensor_copy])
+        w1_mx = quantise("w1", w1_dealt[:])
+        for t in range(PACK):
+            project_a(t)
+        for h in range(2):
+            for t in range(PACK):
+                fetch_partner(t, h * S // 2, S // 2)
+        make_z(0)
+        make_z(1)
+
+        z2_planes = keep.tile([P, PACK, V], BF16, name="z2_planes", tag="kinds0", align_bytes=64)
+        for t in range(PACK):
+            nc.vector.tensor_scalar(z2_planes[:, t, :], placed[t][:], gb_tile[:, t : t + 1], None, ALU.mult)
+        z2_woven = keep.tile([P, PACK * V], BF16, name="z2_woven", align_bytes=64)
+        nc.vector.tensor_copy(
+            z2_woven[:].rearrange("p (c e t) -> p c t e", e=4, t=PACK), z2_planes[:].rearrange("p t (c e) -> p c t e", e=4)
+        )
+        z2_mx = quantise("z2", z2_woven[:])
+        fetch_kinds(1, "w2_dealt")
+
+        score_banks, scores, biases, members = {}, {}, {}, {}
+
+        def score(i):
+            score_banks[i] = psum.tile([P, V], F32, name="bank_b%d" % i)
+            product(score_banks[i], z_mx[i], slice(0, P), z2_mx)
+            scores[i] = keep.tile([P, V], F32, name="s%d" % i)
+            top = keep.tile([P, 1], F32, name="top%d" % i)
+            nc.vector.tensor_scalar(scores[i][:], score_banks[i][:], 0.0625, None, ALU.mult, ALU.max, accum_out=top[:])
+            biases[i] = keep.tile([P, 1], F32, name="bias%d" % i)
+            nc.vector.tensor_scalar(biases[i][:], top[:], tau_tile[:, i : i + 1], -1.0, ALU.mult, ALU.mult)
+
+        def exponentials(i):
+            members[i] = keep.tile([P, G], F32, name="ea%d" % i)
+            for first in range(0, G, EXP_PIECE):
+                offsets = n5_list[:, first // LIST : (first + EXP_PIECE) // LIST]
+                nc.scalar.activation(
+                    members[i][:, first : first + EXP_PIECE], scores[i][:].indirect(offsets), ACT.Exp,
+                    bias=biases[i][:], scale=tau_tile[:, i : i + 1],
+                )
+
+        def halves(view):
+            return view.rearrange("p (h c) -> p h c", h=2)
+
+        def denominate(i, first, count):
+            grouped = members[i][:, 4 * first : 4 * (first + count)].rearrange("p (v m) -> p v m", m=4)
+            sums = twos[:, i % 2, first : first + count, :]
+            nc.vector.tensor_tensor(sums, grouped[:, :, 0:2], grouped[:, :, 2:4], ALU.add)
+            denominators = ring.tile([P, count], F32, name="denominators")
+            nc.vector.scalar_tensor_tensor(denominators[:], sums[:, :, 0], 0.5, sums[:, :, 1], ALU.add, ALU.add)
+            return denominators
+
+        def finish(i, first, count):
+            half, quarter = count // 2, count // 4
+            denominators = denominate(i, first, count)
+            products = ring.tile([P, half], F32, name="products")
+            nc.vector.tensor_tensor(products[:], denominators[:, :half], denominators[:, half:], ALU.mult)
+            numerators = ring.tile([P, count], F32, name="numerators")
+            nc.vector.scalar_tensor_tensor(
+                halves(numerators[:]), halves(score_banks[i][:, first : first + count]), 1.5 * 0.0625,
+                halves(denominators[:])[:, ::-1, :], ALU.mult, ALU.mult,
+            )
+            fours = ring.tile([P, quarter], F32, name="fours")
+            nc.vector.tensor_tensor(fours[:], products[:, :quarter], products[:, quarter:], ALU.mult)
+            inverse_fours = ring.tile([P, quarter], F32, name="inverse_fours")
+            nc.vector.reciprocal(inverse_fours[:], fours[:])
+            inverse_products = ring.tile([P, half], F32, name="inverse_products")
+            nc.vector.tensor_tensor(
+                halves(inverse_products[:]), halves(products[:])[:, ::-1, :],
+                inverse_fours[:].unsqueeze(1).to_broadcast([P, 2, quarter]), ALU.mult,
+            )
+            result = ring.tile([P, count], F32, name="result", bufs=4)
+            nc.vector.tensor_tensor(
+                halves(result[:]), halves(numerators[:]), inverse_products[:].unsqueeze(1).to_broadcast([P, 2, half]), ALU.mult
+            )
+            nc.sync.dma_start(out[i * P : (i + 1) * P, first : first + count], result[:])
+
+        def finish_plainly(i, first, count):
+            denominators = denominate(i, first, count)
+            inverses = keep.tile([P, count], F32, name="inverses")
+            nc.vector.reciprocal(inverses[:], denominators[:])
+            result = ring.tile([P, count], F32, name="result", bufs=4)
+            nc.vector.scalar_tensor_tensor(
+                result[:], score_banks[i][:, first : first + count], 1.5 * 0.0625, inverses[:], ALU.mult, ALU.mult
+            )
+            nc.sync.dma_start(out[i * P : (i + 1) * P, first : first + count], result[:])
+
+        score(0)
+        exponentials(0)
+        score(1)
+        exponentials(1)
+        for i in range(2, ROWS):
+            make_z(i)
+        for i in range(2, ROWS):
+            score(i)
+            exponentials(i)
+        twos = keep.tile([P, 2, V, 2], F32, name="twos", tag="partner")
+        for i in range(ROWS - 1):
+            for first in range(0, V, V // 2):
+                finish(i, first, V // 2)
+        for first in range(0, 3 * V // 4, V // 4):
+            finish(ROWS - 1, first, V // 4)
+        finish_plainly(ROWS - 1, 3 * V // 4, V // 4)

@@ -19,7 +19,7 @@ P = 128
 PACK = 4
 LIST = 16
 ROWS = S // P
-EXP_PIECE = 256
+EXP_PIECE = 512
 
 
 def tile_picked_kqkindgpolaregs_none_p_kernel(
@@ -44,26 +44,30 @@ def tile_picked_kqkindgpolaregs_none_p_kernel(
 
         scale_table = keep.tile([P, T], U8, name="scale_table")
         nc.gpsimd.memset(scale_table[:].bitcast(I32), 0)
-        w2_raw = load_weight("w2_raw", w2)
+        tab_rows = tab.rearrange("(p t) c -> t p c", t=PACK)
+
+        def load_tab(t):
+            tile = keep.tile([P, H], F32, name="tab%d" % t)
+            nc.sync.dma_start(tile[:], tab_rows[t])
+            return tile
+
+        tab_tiles = [load_tab(0)]
         for q in range(4):
             nc.sync.dma_start(
                 scale_table[32 * q : 32 * q + 4, :].bitcast(I32), x_scales[0, 4 * q : 4 * q + 4, :].bitcast(I32)
             )
+        n1_list = load_list("n1_list", n1)
+        tab_tiles.append(load_tab(1))
+        w2_raw = load_weight("w2_raw", w2)
         two_list = load_list("two_list", two)
-        offs_list = load_list("offs_list", offs)
         word_table = keep.tile([P, T], U32, name="word_table")
         nc.sync.dma_start(word_table[:].bitcast(I32), x_words[0].rearrange("p c r -> p (c r)").bitcast(I32))
-        n1_list = load_list("n1_list", n1)
-        tab_rows = tab.rearrange("(p t) c -> t p c", t=PACK)
-        tab_tiles = []
-        for t in range(PACK):
-            tile = keep.tile([P, H], F32, name="tab%d" % t)
-            nc.sync.dma_start(tile[:], tab_rows[t])
-            tab_tiles.append(tile)
+        offs_list = load_list("offs_list", offs)
+        tab_tiles.extend(load_tab(t) for t in range(2, PACK))
         n3_list = load_list("n3_list", n3)
         n4_list = load_list("n4_list", n4)
-        n2_list = load_list("n2_list", n2)
         w1_raw = load_weight("w1_raw", w1)
+        n2_list = load_list("n2_list", n2)
         n5_list = load_list("n5_list", n5)
         tau_tile = keep.tile([P, ROWS], F32, name="tau_tile")
         with nc.allow_non_contiguous_dma(reason="one rate a partition"):
@@ -125,7 +129,13 @@ def tile_picked_kqkindgpolaregs_none_p_kernel(
             nc.vector.tensor_copy(b_tile[:], bank[:])
             b_tiles.append(b_tile)
 
-        pairs, mixed, placed = {}, {}, {}
+        x_offs = (gather_words("offs_words", offs_list, 2), offs_scales)
+        w1_dealt = deal_weight("w1_dealt", w1_raw, [nc.vector.tensor_copy])
+        w1_mx = quantise("w1", w1_dealt[:])
+
+        pairs, placed = {}, {}
+        score_windows = [keep.tile([P, 2 * V], F32, name="score_window%d" % i) for i in range(ROWS)]
+        mixed = w1_dealt[:].bitcast(F32).rearrange("p (t c) -> p t c", t=PACK)
         roots = w2_dealt[:].bitcast(F32).rearrange("p (t c) -> p t c", t=PACK)
 
         def fetch_pairs(t):
@@ -134,20 +144,19 @@ def tile_picked_kqkindgpolaregs_none_p_kernel(
             nc.scalar.activation(pairs[t][:, W:], b_tiles[t][:].indirect(n4_list[:]), ACT.Copy)
 
         def mix_pairs(t):
-            squares = ring.tile([P, 2 * W], F32, name="squares")
-            nc.vector.tensor_tensor(squares[:], pairs[t][:], pairs[t][:], ALU.mult)
-            mixed[t] = keep.tile([P, W], F32, name="rb%d" % t)
-            nc.vector.scalar_tensor_tensor(mixed[t][:], pairs[t][:, :W], -0.5, pairs[t][:, W:], ALU.mult, ALU.add)
-            radicand = keep.tile([P, W], F32, name="radicand%d" % t)
-            nc.vector.scalar_tensor_tensor(radicand[:], squares[:, :W], 0.25, squares[:, W:], ALU.add, ALU.add)
+            squares = score_windows[t][:, V:]
+            nc.gpsimd.tensor_tensor(squares, pairs[t][:], pairs[t][:], ALU.mult)
+            nc.vector.scalar_tensor_tensor(mixed[:, t, :], pairs[t][:, :W], -0.5, pairs[t][:, W:], ALU.mult, ALU.add)
+            radicand = w1_raw[:, t, :W]
+            nc.vector.scalar_tensor_tensor(radicand, squares[:, :W], 0.25, squares[:, W:], ALU.add, ALU.add)
             return radicand
 
         def place_mixed(t):
             placed[t] = keep.tile([P, V], F32, name="dt%d" % t)
-            nc.scalar.activation(placed[t][:].indirect(n4_list[:]), mixed[t][:], ACT.Copy)
+            nc.scalar.activation(placed[t][:].indirect(n4_list[:]), mixed[:, t, :], ACT.Copy)
 
         def root(t, radicand):
-            nc.scalar.activation(roots[:, t, :], radicand[:], ACT.Sqrt)
+            nc.scalar.activation(roots[:, t, :], radicand, ACT.Sqrt)
 
         def place_roots(t):
             nc.scalar.activation(placed[t][:].indirect(n3_list[:]), roots[:, t, :], ACT.Copy)
@@ -166,32 +175,29 @@ def tile_picked_kqkindgpolaregs_none_p_kernel(
 
         kinds = {}
 
-        def fetch_kinds(h, tag):
-            kinds[h] = keep.tile([P, PACK, S // 2], F32, name="kinds%d" % h, tag=tag, align_bytes=64)
-            offsets = n1_list[:, h * S // 2 // LIST : (h + 1) * S // 2 // LIST]
+        def fetch_kinds(first, count, tag):
+            tile = keep.tile([P, PACK, count], F32, name="kinds%d" % first, tag=tag, align_bytes=64)
+            offsets = n1_list[:, first // LIST : (first + count) // LIST]
             for t in range(PACK):
-                nc.scalar.activation(kinds[h][:, t, :], tab_tiles[t][:].indirect(offsets), ACT.Copy)
+                nc.scalar.activation(tile[:, t, :], tab_tiles[t][:].indirect(offsets), ACT.Copy, scale=-2.0)
+            for i in range(first // P, (first + count) // P):
+                kinds[i] = tile[:, :, i * P - first : (i + 1) * P - first]
 
         z_mx = {}
 
-        def make_z(i):
+        def make_z(i, engine, weighted):
             columns = slice(i * P, (i + 1) * P)
-            weighted = keep.tile([P, PACK, P], F32, name="weighted%d" % i, tag="weighted%d" % (i % 2))
-            nc.vector.scalar_tensor_tensor(
-                weighted[:], half_a[:].rearrange("p (t c) -> p t c", t=PACK)[:, :, columns], -2.0,
-                kinds[i // 2][:, :, (i % 2) * P : (i % 2 + 1) * P],
-                ALU.mult, ALU.mult,
-            )
+            engine.tensor_tensor(weighted, half_a[:].rearrange("p (t c) -> p t c", t=PACK)[:, :, columns], kinds[i], ALU.mult)
             z_block = keep.tile([P, PACK * P], BF16, name="z_block%d" % i, tag="z_block%d" % (i % 2), align_bytes=64)
             nc.vector.tensor_tensor(
                 z_block[:].rearrange("p (c e t) -> p c t e", e=4, t=PACK),
-                weighted[:].rearrange("p t (c e) -> p c t e", e=4),
+                weighted.rearrange("p t (c e) -> p c t e", e=4),
                 partner[:, :, columns].rearrange("p t (c e) -> p c t e", e=4),
                 ALU.add,
             )
             z_mx[i] = quantise("z_rows%d" % i, z_block[:])
 
-        fetch_kinds(0, "kinds0")
+        fetch_kinds(0, S - P, "kinds0")
         for t in range(PACK):
             fetch_pairs(t)
         for t in range(PACK):
@@ -201,61 +207,62 @@ def tile_picked_kqkindgpolaregs_none_p_kernel(
             if t > 0:
                 place_roots(t - 1)
         place_roots(PACK - 1)
-        x_offs = (gather_words("offs_words", offs_list, 2), offs_scales)
-        w1_dealt = deal_weight("w1_dealt", w1_raw, [nc.vector.tensor_copy])
-        w1_mx = quantise("w1", w1_dealt[:])
         for t in range(PACK):
             project_a(t)
         for h in range(2):
             for t in range(PACK):
                 fetch_partner(t, h * S // 2, S // 2)
-        make_z(0)
-        make_z(1)
+        for i in range(ROWS - 1):
+            make_z(i, nc.gpsimd, kinds[i])
 
-        z2_planes = keep.tile([P, PACK, V], BF16, name="z2_planes", tag="kinds0", align_bytes=64)
+        z2_pairs = keep.tile([P, 2, V, 2], BF16, name="z2_pairs", tag="kinds0", align_bytes=64)
         for t in range(PACK):
-            nc.vector.tensor_scalar(z2_planes[:, t, :], placed[t][:], gb_tile[:, t : t + 1], None, ALU.mult)
+            nc.vector.tensor_scalar(z2_pairs[:, t // 2, :, t % 2], placed[t][:], gb_tile[:, t : t + 1], None, ALU.mult)
         z2_woven = keep.tile([P, PACK * V], BF16, name="z2_woven", align_bytes=64)
         nc.vector.tensor_copy(
-            z2_woven[:].rearrange("p (c e t) -> p c t e", e=4, t=PACK), z2_planes[:].rearrange("p t (c e) -> p c t e", e=4)
+            z2_woven[:].bitcast(I32).rearrange("p (c e h) -> p c h e", e=4, h=2),
+            z2_pairs[:].rearrange("p h c u -> p (h c u)").bitcast(I32).rearrange("p (h c e) -> p c h e", e=4, h=2),
         )
         z2_mx = quantise("z2", z2_woven[:])
-        fetch_kinds(1, "w2_dealt")
+        fetch_kinds(S - P, P, "w2_dealt")
 
-        score_banks, scores, biases, members = {}, {}, {}, {}
+        negated_tau = keep.tile([P, ROWS], F32, name="negated_tau")
+        nc.gpsimd.tensor_scalar(negated_tau[:], tau_tile[:], -1.0, 0.0, ALU.mult, ALU.add)
+        score_banks, biases, members = {}, {}, {}
 
         def score(i):
             score_banks[i] = psum.tile([P, V], F32, name="bank_b%d" % i)
             product(score_banks[i], z_mx[i], slice(0, P), z2_mx)
-            scores[i] = keep.tile([P, V], F32, name="s%d" % i)
             top = keep.tile([P, 1], F32, name="top%d" % i)
-            nc.vector.tensor_scalar(scores[i][:], score_banks[i][:], 0.0625, None, ALU.mult, ALU.max, accum_out=top[:])
+            nc.vector.tensor_scalar(score_windows[i][:, :V], score_banks[i][:], 0.0625, None, ALU.mult, ALU.max, accum_out=top[:])
             biases[i] = keep.tile([P, 1], F32, name="bias%d" % i)
-            nc.vector.tensor_scalar(biases[i][:], top[:], tau_tile[:, i : i + 1], -1.0, ALU.mult, ALU.mult)
+            nc.scalar.activation(biases[i][:], top[:], ACT.Copy, scale=negated_tau[:, i : i + 1])
 
         def exponentials(i):
             members[i] = keep.tile([P, G], F32, name="ea%d" % i)
             for first in range(0, G, EXP_PIECE):
                 offsets = n5_list[:, first // LIST : (first + EXP_PIECE) // LIST]
                 nc.scalar.activation(
-                    members[i][:, first : first + EXP_PIECE], scores[i][:].indirect(offsets), ACT.Exp,
+                    members[i][:, first : first + EXP_PIECE], score_windows[i][:].indirect(offsets), ACT.Exp,
                     bias=biases[i][:], scale=tau_tile[:, i : i + 1],
                 )
 
         def halves(view):
             return view.rearrange("p (h c) -> p h c", h=2)
 
-        def denominate(i, first, count):
-            grouped = members[i][:, 4 * first : 4 * (first + count)].rearrange("p (v m) -> p v m", m=4)
+        def denominate(i, first, count, engine):
+            grouped = members[i][:].rearrange("p (v m) -> p v m", m=4)
+            for piece in range(first, first + count, EXP_PIECE // 4):
+                columns = slice(piece, piece + EXP_PIECE // 4)
+                engine.tensor_tensor(twos[:, i % 2, columns, :], grouped[:, columns, 0:2], grouped[:, columns, 2:4], ALU.add)
             sums = twos[:, i % 2, first : first + count, :]
-            nc.vector.tensor_tensor(sums, grouped[:, :, 0:2], grouped[:, :, 2:4], ALU.add)
             denominators = ring.tile([P, count], F32, name="denominators")
             nc.vector.scalar_tensor_tensor(denominators[:], sums[:, :, 0], 0.5, sums[:, :, 1], ALU.add, ALU.add)
             return denominators
 
         def finish(i, first, count):
             half, quarter = count // 2, count // 4
-            denominators = denominate(i, first, count)
+            denominators = denominate(i, first, count, nc.gpsimd)
             products = ring.tile([P, half], F32, name="products")
             nc.vector.tensor_tensor(products[:], denominators[:, :half], denominators[:, half:], ALU.mult)
             numerators = ring.tile([P, count], F32, name="numerators")
@@ -279,7 +286,7 @@ def tile_picked_kqkindgpolaregs_none_p_kernel(
             nc.sync.dma_start(out[i * P : (i + 1) * P, first : first + count], result[:])
 
         def finish_plainly(i, first, count):
-            denominators = denominate(i, first, count)
+            denominators = denominate(i, first, count, nc.vector)
             inverses = keep.tile([P, count], F32, name="inverses")
             nc.vector.reciprocal(inverses[:], denominators[:])
             result = ring.tile([P, count], F32, name="result", bufs=4)
@@ -292,11 +299,11 @@ def tile_picked_kqkindgpolaregs_none_p_kernel(
         exponentials(0)
         score(1)
         exponentials(1)
-        for i in range(2, ROWS):
-            make_z(i)
-        for i in range(2, ROWS):
-            score(i)
-            exponentials(i)
+        score(2)
+        exponentials(2)
+        make_z(ROWS - 1, nc.vector, z2_woven[:].bitcast(F32)[:, : PACK * P].rearrange("p (t c) -> p t c", t=PACK))
+        score(ROWS - 1)
+        exponentials(ROWS - 1)
         twos = keep.tile([P, 2, V, 2], F32, name="twos", tag="partner")
         for i in range(ROWS - 1):
             for first in range(0, V, V // 2):

@@ -226,8 +226,6 @@ def tile_picked_kqkindgpolaregs_none_p_kernel(
         z2_mx = quantise("z2", z2_woven[:])
         fetch_kinds(S - P, P, "w2_dealt")
 
-        negated_tau = keep.tile([P, ROWS], F32, name="negated_tau")
-        nc.gpsimd.tensor_scalar(negated_tau[:], tau_tile[:], -1.0, 0.0, ALU.mult, ALU.add)
         score_banks, biases, members = {}, {}, {}
 
         def score(i):
@@ -236,7 +234,7 @@ def tile_picked_kqkindgpolaregs_none_p_kernel(
             top = keep.tile([P, 1], F32, name="top%d" % i)
             nc.vector.tensor_scalar(score_windows[i][:, :V], score_banks[i][:], 0.0625, None, ALU.mult, ALU.max, accum_out=top[:])
             biases[i] = keep.tile([P, 1], F32, name="bias%d" % i)
-            nc.scalar.activation(biases[i][:], top[:], ACT.Copy, scale=negated_tau[:, i : i + 1])
+            nc.gpsimd.tensor_scalar(biases[i][:], top[:], tau_tile[:, i : i + 1], -1.0, ALU.mult, ALU.mult)
 
         def exponentials(i):
             members[i] = keep.tile([P, G], F32, name="ea%d" % i)
@@ -250,45 +248,52 @@ def tile_picked_kqkindgpolaregs_none_p_kernel(
         def halves(view):
             return view.rearrange("p (h c) -> p h c", h=2)
 
-        def denominate(i, first, count, engine):
-            grouped = members[i][:].rearrange("p (v m) -> p v m", m=4)
-            for piece in range(first, first + count, EXP_PIECE // 4):
-                columns = slice(piece, piece + EXP_PIECE // 4)
-                engine.tensor_tensor(twos[:, i % 2, columns, :], grouped[:, columns, 0:2], grouped[:, columns, 2:4], ALU.add)
+        def denominate(i, first, count, denominators):
+            grouped = members[i][:, 4 * first : 4 * (first + count)].rearrange("p (v m) -> p v m", m=4)
             sums = twos[:, i % 2, first : first + count, :]
-            denominators = ring.tile([P, count], F32, name="denominators")
-            nc.vector.scalar_tensor_tensor(denominators[:], sums[:, :, 0], 0.5, sums[:, :, 1], ALU.add, ALU.add)
-            return denominators
+            return denominators, [
+                lambda: nc.vector.tensor_tensor(sums, grouped[:, :, 0:2], grouped[:, :, 2:4], ALU.add),
+                lambda: nc.vector.scalar_tensor_tensor(denominators[:], sums[:, :, 0], 0.5, sums[:, :, 1], ALU.add, ALU.add),
+            ]
 
         def finish(i, first, count):
             half, quarter = count // 2, count // 4
-            denominators = denominate(i, first, count, nc.gpsimd)
+            denominators, front = denominate(i, first, count, ring.tile([P, count], F32, name="denominators"))
             products = ring.tile([P, half], F32, name="products")
-            nc.vector.tensor_tensor(products[:], denominators[:, :half], denominators[:, half:], ALU.mult)
             numerators = ring.tile([P, count], F32, name="numerators")
-            nc.vector.scalar_tensor_tensor(
-                halves(numerators[:]), halves(score_banks[i][:, first : first + count]), 1.5 * 0.0625,
-                halves(denominators[:])[:, ::-1, :], ALU.mult, ALU.mult,
-            )
             fours = ring.tile([P, quarter], F32, name="fours")
-            nc.vector.tensor_tensor(fours[:], products[:, :quarter], products[:, quarter:], ALU.mult)
             inverse_fours = ring.tile([P, quarter], F32, name="inverse_fours")
-            nc.vector.reciprocal(inverse_fours[:], fours[:])
             inverse_products = ring.tile([P, half], F32, name="inverse_products")
-            nc.vector.tensor_tensor(
-                halves(inverse_products[:]), halves(products[:])[:, ::-1, :],
-                inverse_fours[:].unsqueeze(1).to_broadcast([P, 2, quarter]), ALU.mult,
-            )
             result = ring.tile([P, count], F32, name="result", bufs=4)
-            nc.vector.tensor_tensor(
-                halves(result[:]), halves(numerators[:]), inverse_products[:].unsqueeze(1).to_broadcast([P, 2, half]), ALU.mult
-            )
-            nc.sync.dma_start(out[i * P : (i + 1) * P, first : first + count], result[:])
 
-        def finish_plainly(i, first, count):
-            denominators = denominate(i, first, count, nc.vector)
-            inverses = keep.tile([P, count], F32, name="inverses")
-            nc.vector.reciprocal(inverses[:], denominators[:])
+            def divide_and_store():
+                nc.vector.tensor_tensor(
+                    halves(result[:]), halves(numerators[:]),
+                    inverse_products[:].unsqueeze(1).to_broadcast([P, 2, half]), ALU.mult,
+                )
+                nc.sync.dma_start(out[i * P : (i + 1) * P, first : first + count], result[:])
+
+            front = front + [
+                lambda: nc.vector.tensor_tensor(products[:], denominators[:, :half], denominators[:, half:], ALU.mult),
+                lambda: nc.vector.scalar_tensor_tensor(
+                    halves(numerators[:]), halves(score_banks[i][:, first : first + count]), 1.5 * 0.0625,
+                    halves(denominators[:])[:, ::-1, :], ALU.mult, ALU.mult,
+                ),
+            ]
+            back = [
+                lambda: nc.vector.tensor_tensor(fours[:], products[:, :quarter], products[:, quarter:], ALU.mult),
+                lambda: nc.vector.reciprocal(inverse_fours[:], fours[:]),
+                lambda: nc.vector.tensor_tensor(
+                    halves(inverse_products[:]), halves(products[:])[:, ::-1, :],
+                    inverse_fours[:].unsqueeze(1).to_broadcast([P, 2, quarter]), ALU.mult,
+                ),
+                divide_and_store,
+            ]
+            return front, back
+
+        def finish_on_scalar(i, first, count, denominators):
+            inverses = keep.tile([P, count], F32, name="inverses%d" % first)
+            nc.scalar.activation(inverses[:], denominators[:], ACT.Abs_reciprocal_sqrt)
             result = ring.tile([P, count], F32, name="result", bufs=4)
             nc.vector.scalar_tensor_tensor(
                 result[:], score_banks[i][:, first : first + count], 1.5 * 0.0625, inverses[:], ALU.mult, ALU.mult
@@ -305,9 +310,23 @@ def tile_picked_kqkindgpolaregs_none_p_kernel(
         score(ROWS - 1)
         exponentials(ROWS - 1)
         twos = keep.tile([P, 2, V, 2], F32, name="twos", tag="partner")
-        for i in range(ROWS - 1):
-            for first in range(0, V, V // 2):
-                finish(i, first, V // 2)
-        for first in range(0, 3 * V // 4, V // 4):
-            finish(ROWS - 1, first, V // 4)
-        finish_plainly(ROWS - 1, 3 * V // 4, V // 4)
+        chunks = [(i, first, V // 2) for i in range(ROWS - 1) for first in range(0, V, V // 2)]
+        pending = [lambda: None] * 4
+        for chunk in chunks:
+            front, back = finish(*chunk)
+            for step, earlier in zip(front, pending):
+                step()
+                earlier()
+            pending = back
+        last = []
+        for first, count in ((0, V // 2), (V // 2, V // 4), (3 * V // 4, V // 4)):
+            denominators, front = denominate(ROWS - 1, first, count, keep.tile([P, count], F32, name="last_denominators%d" % first))
+            squared = keep.tile([P, count], F32, name="squared%d" % first)
+            last.append((first, count, squared))
+            for step, earlier in zip(front, pending):
+                step()
+                earlier()
+            pending = pending[len(front) :] + [lambda: None] * len(front)
+            nc.vector.tensor_tensor(squared[:], denominators[:], denominators[:], ALU.mult)
+        for first, count, denominators in last:
+            finish_on_scalar(ROWS - 1, first, count, denominators)

@@ -42,6 +42,10 @@ def tile_picked_kqkindgpolaregs_none_p_kernel(
             nc.sync.dma_start(tile[:], source.rearrange("(p j) c -> p j c", j=PACK))
             return tile
 
+        warm_up = keep.tile([P, 2], F32, name="warm_up")
+        nc.vector.memset(warm_up[:, 0:1], 1.0)
+        nc.scalar.activation(warm_up[:, 1:2], warm_up[:, 0:1], ACT.Sqrt)
+
         scale_table = keep.tile([P, T], U8, name="scale_table")
         nc.gpsimd.memset(scale_table[:].bitcast(I32), 0)
         tab_rows = tab.rearrange("(p t) c -> t p c", t=PACK)

from contextlib import ExitStack

import concourse.mybir as mybir

K, T, S, V, H, W, G = 512, 2048, 512, 512, 512, 256, 2048
FLOPS = 2 * K * H * S + 2 * K * H * V + 2 * H * S * V

F32 = mybir.dt.float32
BF16 = mybir.dt.bfloat16
I32 = mybir.dt.int32
U32 = mybir.dt.uint32
U16 = mybir.dt.uint16
U8 = mybir.dt.uint8
FP8X4 = mybir.dt.float8_e4m3fn_x4
ALU = mybir.AluOpType
ACT = mybir.ActivationFunctionType

P = 128
PACK = 4
LIST = 16
ROWS = S // P
EXP_PIECE = 512


def tile_picked_kqkindgpolaregs_none_p_kernel(
    tc, x_words, x_scales, w1, w2, tab, ga, gb, tau, offs, two, n1, n2, n3, n4, n5, out
):
    nc = tc.nc
    with ExitStack() as ctx:
        lists = ctx.enter_context(tc.tile_pool(name="lists", bufs=1))
        keep = ctx.enter_context(tc.tile_pool(name="keep", bufs=1))
        ring = ctx.enter_context(tc.tile_pool(name="ring", bufs=2))
        psum = ctx.enter_context(tc.psum_pool(name="psum", bufs=1))

        def load_list(name, source):
            tile = lists.tile([P, source.shape[1]], U16, name=name)
            nc.sync.dma_start(tile[:], source)
            return tile

        def load_weight(name, source):
            tile = keep.tile([P, PACK, H], F32, name=name)
            nc.sync.dma_start(tile[:], source.rearrange("(p j) c -> p j c", j=PACK))
            return tile

        warm_up = keep.tile([P, 2], F32, name="warm_up")
        nc.vector.memset(warm_up[:, 0:1], 1.0)
        nc.scalar.activation(warm_up[:, 1:2], warm_up[:, 0:1], ACT.Sqrt)

        scale_table = keep.tile([P, T], U8, name="scale_table")
        nc.gpsimd.memset(scale_table[:].bitcast(I32), 0)
        tab_rows = tab.rearrange("(p t) c -> t p c", t=PACK)

        def load_tab(t):
            tile = keep.tile([P, H], F32, name="tab%d" % t)
            nc.sync.dma_start(tile[:], tab_rows[t])
            return tile

        tab_tiles = [load_tab(0)]
        for q in range(4):
            nc.sync.dma_start(
                scale_table[32 * q : 32 * q + 4, :].bitcast(I32), x_scales[0, 4 * q : 4 * q + 4, :].bitcast(I32)
            )
        n1_list = load_list("n1_list", n1)
        tab_tiles.append(load_tab(1))
        w2_raw = load_weight("w2_raw", w2)
        two_list = load_list("two_list", two)
        word_table = keep.tile([P, T], U32, name="word_table")
        nc.sync.dma_start(word_table[:].bitcast(I32), x_words[0].rearrange("p c r -> p (c r)").bitcast(I32))
        offs_list = load_list("offs_list", offs)
        tab_tiles.extend(load_tab(t) for t in range(2, PACK))
        n3_list = load_list("n3_list", n3)
        n4_list = load_list("n4_list", n4)
        w1_raw = load_weight("w1_raw", w1)
        n2_list = load_list("n2_list", n2)
        n5_list = load_list("n5_list", n5)
        tau_tile = keep.tile([P, ROWS], F32, name="tau_tile")
        with nc.allow_non_contiguous_dma(reason="one rate a partition"):
            nc.sync.dma_start(tau_tile[:], tau.rearrange("(i p) o -> p (i o)", p=P))
        ga_tile = keep.tile([P, PACK], F32, name="ga_tile")
        nc.gpsimd.dma_start(ga_tile[:], ga.rearrange("(p t) o -> p (t o)", t=PACK))
        gb_tile = keep.tile([P, PACK], F32, name="gb_tile")
        nc.gpsimd.dma_start(gb_tile[:], gb.rearrange("(p t) o -> p (t o)", t=PACK))

        def gather_scales(name, offsets):
            tile = keep.tile([P, S], U8, name=name, align_bytes=64)
            nc.vector.tensor_copy(tile[:], scale_table[:].indirect(offsets[:]))
            return tile

        def gather_words(name, offsets, pieces):
            tile = keep.tile([P, S], U32, name=name, align_bytes=64)
            for first in range(0, S, S // pieces):
                columns = slice(first // LIST, (first + S // pieces) // LIST)
                nc.vector.tensor_copy(tile[:, first : first + S // pieces], word_table[:].indirect(offsets[:, columns]))
            return tile

        def deal_weight(name, raw, copies):
            dealt = keep.tile([P, PACK * H], BF16, name=name, tag=name, align_bytes=64)
            view = dealt[:].rearrange("p (t m j) -> p m j t", t=PACK, j=PACK)
            source = raw[:].rearrange("p j (m t) -> p m j t", t=PACK)
            share = P // len(copies)
            for h, copy in enumerate(copies):
                copy(view[:, h * share : (h + 1) * share], source[:, h * share : (h + 1) * share])
            return dealt

        def quantise(name, values):
            width = values.shape[1] // PACK
            codes = keep.tile([P, width], U32, name=name + "_codes", align_bytes=64)
            scales = keep.tile([P, width], U8, name=name + "_scales", align_bytes=64)
            nc.vector.quantize_mx(out=codes[:].bitcast(FP8X4), scales=scales[:], in_=values)
            return codes, scales

        def product(bank, left, left_columns, right):
            nc.tensor.matmul_mx(
                out=bank[:],
                lhsT=left[0][:, left_columns].bitcast(FP8X4),
                lhsT_scale=left[1][:, left_columns],
                rhs=right[0][:].bitcast(FP8X4),
                rhs_scale=right[1][:],
                start=True,
                stop=True,
            )

        two_scales = gather_scales("two_scales", two_list)
        w2_dealt = deal_weight("w2_dealt", w2_raw, [nc.scalar.copy, nc.vector.tensor_copy])
        offs_scales = gather_scales("offs_scales", offs_list)
        w2_mx = quantise("w2", w2_dealt[:])
        x_two = (gather_words("two_words", two_list, 1), two_scales)
        b_tiles = []
        for t in range(PACK):
            bank = psum.tile([P, V], F32, name="bank_b%d" % t)
            product(bank, w2_mx, slice(t * P, (t + 1) * P), x_two)
            b_tile = keep.tile([P, V], F32, name="b%d" % t)
            nc.vector.tensor_copy(b_tile[:], bank[:])
            b_tiles.append(b_tile)

        x_offs = (gather_words("offs_words", offs_list, 2), offs_scales)
        w1_dealt = deal_weight("w1_dealt", w1_raw, [nc.vector.tensor_copy])
        w1_mx = quantise("w1", w1_dealt[:])

        pairs, placed = {}, {}
        score_windows = [keep.tile([P, 2 * V], F32, name="score_window%d" % i) for i in range(ROWS)]
        mixed = w1_dealt[:].bitcast(F32).rearrange("p (t c) -> p t c", t=PACK)
        roots = w2_dealt[:].bitcast(F32).rearrange("p (t c) -> p t c", t=PACK)

        def fetch_pairs(t):
            pairs[t] = keep.tile([P, 2 * W], F32, name="pairs%d" % t)
            nc.scalar.activation(pairs[t][:, :W], b_tiles[t][:].indirect(n3_list[:]), ACT.Copy)
            nc.scalar.activation(pairs[t][:, W:], b_tiles[t][:].indirect(n4_list[:]), ACT.Copy)

        def mix_pairs(t):
            squares = score_windows[t][:, V:]
            nc.gpsimd.tensor_tensor(squares, pairs[t][:], pairs[t][:], ALU.mult)
            nc.vector.scalar_tensor_tensor(mixed[:, t, :], pairs[t][:, :W], -0.5, pairs[t][:, W:], ALU.mult, ALU.add)
            radicand = w1_raw[:, t, :W]
            nc.vector.scalar_tensor_tensor(radicand, squares[:, :W], 0.25, squares[:, W:], ALU.add, ALU.add)
            return radicand

        def place_mixed(t):
            placed[t] = keep.tile([P, V], F32, name="dt%d" % t)
            nc.scalar.activation(placed[t][:].indirect(n4_list[:]), mixed[:, t, :], ACT.Copy)

        def root(t, radicand):
            nc.scalar.activation(roots[:, t, :], radicand, ACT.Sqrt)

        def place_roots(t):
            nc.scalar.activation(placed[t][:].indirect(n3_list[:]), roots[:, t, :], ACT.Copy)

        half_a = keep.tile([P, PACK * S], F32, name="half_a")
        partner = keep.tile([P, PACK, S], F32, name="partner", tag="partner")

        def project_a(t):
            bank = psum.tile([P, S], F32, name="bank_a%d" % t)
            product(bank, w1_mx, slice(t * P, (t + 1) * P), x_offs)
            nc.vector.tensor_scalar(half_a[:, t * S : (t + 1) * S], bank[:], ga_tile[:, t : t + 1], -0.5, ALU.mult, ALU.mult)

        def fetch_partner(t, first, count):
            offsets = n2_list[:, first // LIST : (first + count) // LIST]
            nc.vector.tensor_copy(partner[:, t, first : first + count], half_a[:, t * S : (t + 1) * S].indirect(offsets))

        kinds = {}

        def fetch_kinds(first, count, tag):
            tile = keep.tile([P, PACK, count], F32, name="kinds%d" % first, tag=tag, align_bytes=64)
            offsets = n1_list[:, first // LIST : (first + count) // LIST]
            for t in range(PACK):
                nc.scalar.activation(tile[:, t, :], tab_tiles[t][:].indirect(offsets), ACT.Copy, scale=-2.0)
            for i in range(first // P, (first + count) // P):
                kinds[i] = tile[:, :, i * P - first : (i + 1) * P - first]

        z_mx = {}

        def make_z(i, engine, weighted):
            columns = slice(i * P, (i + 1) * P)
            engine.tensor_tensor(weighted, half_a[:].rearrange("p (t c) -> p t c", t=PACK)[:, :, columns], kinds[i], ALU.mult)
            z_block = keep.tile([P, PACK * P], BF16, name="z_block%d" % i, tag="z_block%d" % (i % 2), align_bytes=64)
            nc.vector.tensor_tensor(
                z_block[:].rearrange("p (c e t) -> p c t e", e=4, t=PACK),
                weighted.rearrange("p t (c e) -> p c t e", e=4),
                partner[:, :, columns].rearrange("p t (c e) -> p c t e", e=4),
                ALU.add,
            )
            z_mx[i] = quantise("z_rows%d" % i, z_block[:])

        fetch_kinds(0, S - P, "kinds0")
        for t in range(PACK):
            fetch_pairs(t)
        for t in range(PACK):
            radicand = mix_pairs(t)
            place_mixed(t)
            root(t, radicand)
            if t > 0:
                place_roots(t - 1)
        place_roots(PACK - 1)
        for t in range(PACK):
            project_a(t)
        for h in range(2):
            for t in range(PACK):
                fetch_partner(t, h * S // 2, S // 2)
        for i in range(ROWS - 1):
            make_z(i, nc.gpsimd, kinds[i])

        z2_pairs = keep.tile([P, 2, V, 2], BF16, name="z2_pairs", tag="kinds0", align_bytes=64)
        for t in range(PACK):
            nc.vector.tensor_scalar(z2_pairs[:, t // 2, :, t % 2], placed[t][:], gb_tile[:, t : t + 1], None, ALU.mult)
        z2_woven = keep.tile([P, PACK * V], BF16, name="z2_woven", align_bytes=64)
        nc.vector.tensor_copy(
            z2_woven[:].bitcast(I32).rearrange("p (c e h) -> p c h e", e=4, h=2),
            z2_pairs[:].rearrange("p h c u -> p (h c u)").bitcast(I32).rearrange("p (h c e) -> p c h e", e=4, h=2),
        )
        z2_mx = quantise("z2", z2_woven[:])
        fetch_kinds(S - P, P, "w2_dealt")

        score_banks, biases, members = {}, {}, {}

        def score(i):
            score_banks[i] = psum.tile([P, V], F32, name="bank_b%d" % i)
            product(score_banks[i], z_mx[i], slice(0, P), z2_mx)
            top = keep.tile([P, 1], F32, name="top%d" % i)
            nc.vector.tensor_scalar(score_windows[i][:, :V], score_banks[i][:], 0.0625, None, ALU.mult, ALU.max, accum_out=top[:])
            biases[i] = keep.tile([P, 1], F32, name="bias%d" % i)
            nc.gpsimd.tensor_scalar(biases[i][:], top[:], tau_tile[:, i : i + 1], -1.0, ALU.mult, ALU.mult)

        def exponentials(i):
            members[i] = keep.tile([P, G], F32, name="ea%d" % i)
            for first in range(0, G, EXP_PIECE):
                offsets = n5_list[:, first // LIST : (first + EXP_PIECE) // LIST]
                nc.scalar.activation(
                    members[i][:, first : first + EXP_PIECE], score_windows[i][:].indirect(offsets), ACT.Exp,
                    bias=biases[i][:], scale=tau_tile[:, i : i + 1],
                )

        def halves(view):
            return view.rearrange("p (h c) -> p h c", h=2)

        def denominate(i, first, count, denominators):
            grouped = members[i][:, 4 * first : 4 * (first + count)].rearrange("p (v m) -> p v m", m=4)
            sums = twos[:, i % 2, first : first + count, :]
            return denominators, [
                lambda: nc.vector.tensor_tensor(sums, grouped[:, :, 0:2], grouped[:, :, 2:4], ALU.add),
                lambda: nc.vector.scalar_tensor_tensor(denominators[:], sums[:, :, 0], 0.5, sums[:, :, 1], ALU.add, ALU.add),
            ]

        def finish(i, first, count):
            half, quarter = count // 2, count // 4
            denominators, front = denominate(i, first, count, ring.tile([P, count], F32, name="denominators"))
            products = ring.tile([P, half], F32, name="products")
            numerators = ring.tile([P, count], F32, name="numerators")
            fours = ring.tile([P, quarter], F32, name="fours")
            inverse_fours = ring.tile([P, quarter], F32, name="inverse_fours")
            inverse_products = ring.tile([P, half], F32, name="inverse_products")
            result = ring.tile([P, count], F32, name="result", bufs=4)

            def divide_and_store():
                nc.vector.tensor_tensor(
                    halves(result[:]), halves(numerators[:]),
                    inverse_products[:].unsqueeze(1).to_broadcast([P, 2, half]), ALU.mult,
                )
                nc.sync.dma_start(out[i * P : (i + 1) * P, first : first + count], result[:])

            front = front + [
                lambda: nc.vector.tensor_tensor(products[:], denominators[:, :half], denominators[:, half:], ALU.mult),
                lambda: nc.vector.scalar_tensor_tensor(
                    halves(numerators[:]), halves(score_banks[i][:, first : first + count]), 1.5 * 0.0625,
                    halves(denominators[:])[:, ::-1, :], ALU.mult, ALU.mult,
                ),
            ]
            back = [
                lambda: nc.vector.tensor_tensor(fours[:], products[:, :quarter], products[:, quarter:], ALU.mult),
                lambda: nc.vector.reciprocal(inverse_fours[:], fours[:]),
                lambda: nc.vector.tensor_tensor(
                    halves(inverse_products[:]), halves(products[:])[:, ::-1, :],
                    inverse_fours[:].unsqueeze(1).to_broadcast([P, 2, quarter]), ALU.mult,
                ),
                divide_and_store,
            ]
            return front, back

        def finish_on_scalar(i, first, count, denominators):
            inverses = keep.tile([P, count], F32, name="inverses%d" % first)
            nc.scalar.activation(inverses[:], denominators[:], ACT.Abs_reciprocal_sqrt)
            result = ring.tile([P, count], F32, name="result", bufs=4)
            nc.vector.scalar_tensor_tensor(
                result[:], score_banks[i][:, first : first + count], 1.5 * 0.0625, inverses[:], ALU.mult, ALU.mult
            )
            nc.sync.dma_start(out[i * P : (i + 1) * P, first : first + count], result[:])

        score(0)
        exponentials(0)
        score(1)
        exponentials(1)
        score(2)
        exponentials(2)
        make_z(ROWS - 1, nc.vector, z2_woven[:].bitcast(F32)[:, : PACK * P].rearrange("p (t c) -> p t c", t=PACK))
        score(ROWS - 1)
        exponentials(ROWS - 1)
        twos = keep.tile([P, 2, V, 2], F32, name="twos", tag="partner")
        chunks = [(i, first, V // 2) for i in range(ROWS - 1) for first in range(0, V, V // 2)]
        pending = [lambda: None] * 4
        for chunk in chunks:
            front, back = finish(*chunk)
            for step, earlier in zip(front, pending):
                step()
                earlier()
            pending = back
        last = []
        for first, count in ((0, V // 2), (V // 2, V // 4), (3 * V // 4, V // 4)):
            denominators, front = denominate(ROWS - 1, first, count, keep.tile([P, count], F32, name="last_denominators%d" % first))
            squared = keep.tile([P, count], F32, name="squared%d" % first)
            last.append((first, count, squared))
            for step, earlier in zip(front, pending):
                step()
                earlier()
            pending = pending[len(front) :] + [lambda: None] * len(front)
            nc.vector.tensor_tensor(squared[:], denominators[:], denominators[:], ALU.mult)
        for first, count, denominators in last:
            finish_on_scalar(ROWS - 1, first, count, denominators)
